import numpy as np
import ml_dtypes


def mxq(x, axis, fmt="e4m3"):
    dtype, down = {"e4m3": (ml_dtypes.float8_e4m3fn, 7), "e5m2": (ml_dtypes.float8_e5m2, 14)}[fmt]
    v = np.moveaxis(np.asarray(x, np.float32).astype(ml_dtypes.bfloat16).astype(np.float64), axis, -1)
    blocks = v.reshape(v.shape[:-1] + (-1, 32))
    amax = np.abs(blocks).max(-1, keepdims=True)
    byte = np.maximum(np.where(amax > 0, np.frexp(amax)[1] - 1 + 127, 0) - down, 1)
    scale = np.exp2(byte - 127.0)
    codes = (blocks / scale).astype(np.float32).astype(dtype).astype(np.float64)
    return np.moveaxis((codes * scale).reshape(v.shape), -1, axis)


WIDE = False


def mx_kscale(k):
    if not WIDE:
        return np.ones(k)
    levels = np.array([10, -10, 5, -5, 0])
    if k % 512:
        return np.exp2(np.random.permutation(np.resize(levels, k // 32))).repeat(32)
    a = np.empty((k // 512, 16))
    for p in range(k // 512):
        a[p, :8] = np.random.permutation(np.resize(levels, 8))
        for g in range(8):
            far = levels[np.abs(levels - a[p, g]) >= 10]
            a[p, g + 8] = far[np.random.randint(len(far))]
    return np.exp2(a.ravel()).repeat(32)


def f64(x):
    return np.asarray(x).astype(np.float64)


def striped(idx):
    return np.tile(idx.reshape(-1, 16).T, (8, 1)).astype(np.uint16)


def unstriped(offs):
    return offs[:16].T.reshape(-1).astype(np.int64)


def striped8(idx):
    return np.concatenate([x.reshape(-1, 16).T for x in idx]).astype(np.uint16)


def runs(offs, k):
    lists = np.stack([offs[16 * r : 16 * r + 16].T.reshape(-1) for r in range(8)]).astype(np.int64)
    return lists[np.arange(k) % 512 // 64]


def pack_weight(w):
    k, n = w.shape
    w = f64(np.asarray(w, np.float32).astype(ml_dtypes.bfloat16)).reshape(k // 32, 32, n)
    amax = np.abs(w).max(1)
    byte = np.clip(np.where(amax > 0, np.frexp(amax)[1] - 1 + 127 - 7, 1), 1, 254)
    scaled = (w * np.exp2(127.0 - byte)[:, None, :]).reshape(k, n).astype(np.float32)
    words = np.ascontiguousarray(scaled.reshape(k // 512, 128, 4, n).transpose(0, 1, 3, 2)).astype(ml_dtypes.float8_e4m3fn).view(np.uint8)
    return words, np.ascontiguousarray(byte.astype(np.uint8).reshape(k // 512, 16, n))


def unpack_weight(words, scales):
    g, p, n, _ = words.shape
    vals = np.ascontiguousarray(words).view(ml_dtypes.float8_e4m3fn).astype(np.float64) * np.repeat(np.exp2(scales.astype(np.float64) - 127.0), 8, axis=1)[..., None]
    return vals.transpose(0, 1, 3, 2).reshape(g * 512, n)


def relu(v):
    return np.maximum(v, 0.0)


def sigmoid(v):
    return 1.0 / (1.0 + np.exp(-np.maximum(v, -700.0)))

def planes(y):
    n, m = y.shape
    v = y.astype(np.float32).astype(ml_dtypes.bfloat16).astype(np.float64).reshape(n // 32, 32, m)
    top = np.abs(v).max(1)
    byte = np.clip(np.where(top > 0, np.frexp(top)[1] - 1 + 127 - 7, 1), 1, 254)
    codes = (v * np.exp2(127.0 - byte)[:, None, :]).reshape(n, m).astype(np.float32).astype(ml_dtypes.float8_e4m3fn).view(np.uint8)
    words = codes.reshape(n // 512, 128, 4, m).transpose(0, 1, 3, 2)
    return np.ascontiguousarray(words), np.ascontiguousarray(byte.astype(np.uint8).reshape(n // 512, 16, m))


K, T, S, G, H, W = 512, 1024, 256, 2048, 512, 192


def setup_inputs():
    n = np.random.standard_normal
    s = mx_kscale(K)[:, None]
    packed_xT = pack_weight(n((K, T)) * s)
    packed_dT = pack_weight(n((K, G)) / s)
    return {
        "x_words": packed_xT[0],
        "x_scales": packed_xT[1],
        "d_words": packed_dT[0],
        "d_scales": packed_dT[1],
        "gs": (np.random.uniform(0.5, 1.5, (K, 1)) * s).astype(np.float32),
        "offs": striped(np.random.permutation(T)[:S]),
        "k1": striped8(np.random.randint(0, G, (8, H))),
        "n1": striped(np.random.permutation(S)[:W]),
        "n2": striped(np.random.permutation(S)[:W]),
        "k2": striped8(np.random.randint(0, G, (8, H))),
        "n3": striped8(np.stack([np.random.permutation(S) for _ in range(8)])),
        "n4": striped8(np.stack([np.random.permutation(S) for _ in range(8)])),
    }


def reference(x_words, x_scales, d_words, d_scales, gs, offs, k1, n1, n2, k2, n3, n4):
    d_k2 = unpack_weight(d_words, d_scales)[np.arange(K)[:, None], runs(k2, K)]
    d_k1 = unpack_weight(d_words, d_scales)[np.arange(K)[:, None], runs(k1, K)]
    xq = unpack_weight(x_words, x_scales)[:, unstriped(offs)]
    h = 0.0625 * (d_k1.T @ xq)
    old = h[:, unstriped(n1)]
    pa = h[:, unstriped(n2)]
    ra = old * sigmoid(pa)
    ds = h.copy()
    ds[:, unstriped(n1)] = ra
    z = f64(gs) * ds
    h2 = 0.0625 * ((d_k2.T @ mxq(z, 0, "e4m3")))
    out_0 = relu(h2 - (h2[np.arange(H)[:, None], runs(n3, H)])) + 0.5 * (relu(h2[np.arange(H)[:, None], runs(n4, H)] - h2))
    return (out_0,) + planes(out_0)

@@ -1,0 +1,232 @@
+from contextlib import ExitStack
+
+import concourse.mybir as mybir
+
+K, T, S, G, H, W = 512, 1024, 256, 2048, 512, 192
+FLOPS = 2 * 2 * K * H * S
+
+F32 = mybir.dt.float32
+BF16 = mybir.dt.bfloat16
+I32 = mybir.dt.int32
+U32 = mybir.dt.uint32
+U16 = mybir.dt.uint16
+U8 = mybir.dt.uint8
+FP8X4 = mybir.dt.float8_e4m3fn_x4
+ALU = mybir.AluOpType
+ACT = mybir.ActivationFunctionType
+
+P = 128
+PACK = 4
+HALF = S // 2
+H_WINDOW = 2 * W
+
+
+def tile_picked_codekgatehinge_none_po_kernel(
+    tc, x_words, x_scales, d_words, d_scales, gs, offs, k1, n1, n2, k2, n3, n4, out_0, out_1, out_2
+):
+    nc = tc.nc
+    with ExitStack() as ctx:
+        lists = ctx.enter_context(tc.tile_pool(name="lists", bufs=1))
+        keep = ctx.enter_context(tc.tile_pool(name="keep", bufs=1))
+        psum = ctx.enter_context(tc.psum_pool(name="psum", bufs=1))
+
+        def load_list(name, src):
+            t = lists.tile([P, src.shape[1]], U16, name=name)
+            nc.sync.dma_start(t[:], src)
+            return t
+
+        def sb(name, shape, dtype, tag=None):
+            return keep.tile(shape, dtype, name=name, tag=tag or name, align_bytes=64)
+
+        d_scale_table = sb("d_scale_table", [P, G], U8)
+        x_scale_table = sb("x_scale_table", [P, T], U8)
+        d_word_table = sb("d_word_table", [P, G], U32)
+        x_word_table = sb("x_word_table", [P, T], U32)
+
+        def load_scale_table(table, rows):
+            width = rows.shape[1] // 4
+            nc.scalar.dma_start(table[:].bitcast(I32), rows.bitcast(I32).unsqueeze(1).to_broadcast([16, 8, width]))
+
+        k1_list = load_list("k1_list", k1)
+        load_scale_table(d_scale_table, d_scales[0])
+        offs_list = load_list("offs_list", offs)
+        load_scale_table(x_scale_table, x_scales[0])
+        nc.sync.dma_start(d_word_table[:].bitcast(I32), d_words[0].rearrange("p n t -> p (n t)").bitcast(I32))
+        n2_list = load_list("n2_list", n2)
+        nc.sync.dma_start(x_word_table[:].bitcast(I32), x_words[0].rearrange("p n t -> p (n t)").bitcast(I32))
+        n1_list = load_list("n1_list", n1)
+        k2_list = load_list("k2_list", k2)
+        n3_list = load_list("n3_list", n3)
+        n4_list = load_list("n4_list", n4)
+        gain = sb("gain", [P, PACK], F32)
+        nc.gpsimd.dma_start(gain[:], gs.rearrange("(p t) o -> p (t o)", t=PACK))
+
+        h = [sb(f"h{t}", [P, H_WINDOW], F32) for t in range(PACK)]
+        for t in range(PACK):
+            nc.vector.memset(h[t][:, S:], 0.0)
+
+        def place_rows(plane, queue):
+            for j in range(1, 4):
+                queue.dma_start(plane[j:P:32, :].bitcast(I32), plane[8 * j : P : 32, :].bitcast(I32))
+
+        def coded_scales(name, codes, pieces, plane, tag=None):
+            picked = sb(name + "_picked", [P, H], U8, tag)
+            cols = H // 16 // pieces
+            for i in range(pieces):
+                nc.vector.tensor_copy(
+                    picked[:, 16 * cols * i : 16 * cols * (i + 1)],
+                    d_scale_table[:].indirect(codes[:, cols * i : cols * (i + 1)]),
+                )
+            nc.vector.tensor_copy(
+                plane[:, :H].rearrange("p (t m) -> p t m", t=PACK), picked[:].rearrange("p (m t) -> p t m", t=PACK)
+            )
+
+        def coded_words(name, codes, pieces, tag=None):
+            picked = sb(name + "_picked", [P, H], U32, tag)
+            cols = H // 16 // pieces
+            for i in range(pieces):
+                nc.vector.tensor_copy(
+                    picked[:, 16 * cols * i : 16 * cols * (i + 1)],
+                    d_word_table[:].indirect(codes[:, cols * i : cols * (i + 1)]),
+                )
+            return picked
+
+        def deal_words(words, picked, first, last):
+            nc.vector.tensor_copy(
+                words[:].bitcast(I32).rearrange("p (t m) -> p t m", t=PACK)[:, first:last, :],
+                picked[:].bitcast(I32).rearrange("p (m t) -> p t m", t=PACK)[:, first:last, :],
+            )
+
+        plane1 = sb("plane1", [P, H + S], U8, "plane1")
+        coded_scales("w1_scales", k1_list, 1, plane1)
+        xq_picked = sb("xq_picked", [P, S], U8)
+        nc.vector.tensor_copy(xq_picked[:], x_scale_table[:].indirect(offs_list[:]))
+        nc.vector.tensor_copy(plane1[:, H:].bitcast(I32), xq_picked[:].bitcast(I32))
+        place_rows(plane1, nc.scalar)
+        w1_picked = coded_words("w1_words", k1_list, 1)
+        w1_words = sb("w1_words", [P, H], U32)
+        deal_words(w1_words, w1_picked, 0, PACK)
+        xq_words = sb("xq_words", [P, S], U32)
+        nc.vector.tensor_copy(xq_words[:], x_word_table[:].indirect(offs_list[:]))
+
+        for t in range(PACK):
+            cols = slice(t * P, (t + 1) * P)
+            acc = psum.tile([P, S], F32, name=f"acc1_{t}")
+            nc.tensor.matmul_mx(
+                out=acc[:],
+                lhsT=w1_words[:, cols].bitcast(FP8X4),
+                lhsT_scale=plane1[:, cols],
+                rhs=xq_words[:].bitcast(FP8X4),
+                rhs_scale=plane1[:, H:],
+                start=True,
+                stop=True,
+            )
+            nc.vector.tensor_scalar(h[t][:, :S], acc[:], 0.0625, None, ALU.mult)
+
+        z = [sb(f"z{c}", [P, HALF, PACK], BF16) for c in range(2)]
+
+        def fetch(t):
+            gate = sb(f"gate{t}", [P, W], F32)
+            old = sb(f"old{t}", [P, W], F32)
+            ra = sb(f"ra{t}", [P, W], F32)
+            nc.scalar.activation(gate[:], h[t][:].indirect(n2_list[:]), ACT.Sigmoid)
+            nc.scalar.activation(old[:], h[t][:].indirect(n1_list[:]), ACT.Copy)
+            nc.vector.tensor_tensor(ra[:], old[:], gate[:], ALU.mult)
+            return ra
+
+        def put(t, ra):
+            nc.scalar.activation(h[t][:].indirect(n1_list[:]), ra[:], ACT.Copy)
+            for c in range(2):
+                nc.vector.tensor_scalar(
+                    z[c][:, :, t], h[t][:, c * HALF : (c + 1) * HALF], gain[:, t : t + 1], None, ALU.mult
+                )
+
+        ras = [fetch(0)]
+        for t in range(1, PACK):
+            ras.append(fetch(t))
+            put(t - 1, ras[t - 1])
+        put(PACK - 1, ras[PACK - 1])
+
+        w2_scales = sb("w2_scales", [P, H], U8)
+        coded_scales("w2_scales", k2_list, 2, w2_scales, "plane1")
+        place_rows(w2_scales, nc.sync)
+        w2_picked = coded_words("w2_words", k2_list, 2, "w1_words")
+        w2_words = sb("w2_words", [P, H], U32)
+        deal_words(w2_words, w2_picked, 0, PACK)
+
+        z_words = sb("z_words", [P, S], U32)
+        z_scales = sb("z_scales", [P, S], U8)
+        for c in range(2):
+            cols = slice(c * HALF, (c + 1) * HALF)
+            nc.vector.quantize_mx(
+                out=z_words[:, cols].bitcast(FP8X4), scales=z_scales[:, cols], in_=z[c][:].rearrange("p n t -> p (n t)")
+            )
+
+        h2 = [sb(f"h2_{t}", [P, S], F32) for t in range(PACK)]
+        acc2 = [psum.tile([P, S], F32, name=f"acc2_{t}") for t in range(PACK)]
+        for t in range(PACK):
+            cols = slice(t * P, (t + 1) * P)
+            nc.tensor.matmul_mx(
+                out=acc2[t][:],
+                lhsT=w2_words[:, cols].bitcast(FP8X4),
+                lhsT_scale=w2_scales[:, cols],
+                rhs=z_words[:].bitcast(FP8X4),
+                rhs_scale=z_scales[:],
+                start=True,
+                stop=True,
+            )
+            if t == 0:
+                nc.scalar.activation(h2[t][:], acc2[t][:], ACT.Copy, scale=0.0625)
+            else:
+                nc.vector.tensor_scalar(h2[t][:], acc2[t][:], 0.0625, None, ALU.mult)
+
+        out_rows = out_0.rearrange("(p t) s -> p t s", t=PACK)
+        y = [sb(f"y{c}", [P, PACK, HALF], F32) for c in range(2)]
+        rounded = sb("rounded", [P, S, PACK], BF16)
+
+        def differences(c, t):
+            cols = slice(c * HALF, (c + 1) * HALF)
+            entries = slice(c * HALF // 16, (c + 1) * HALF // 16)
+            low = sb(f"low{c}{t}", [P, HALF], F32)
+            high = sb(f"high{c}{t}", [P, HALF], F32)
+            up = sb(f"up{c}{t}", [P, HALF], F32)
+            down = sb(f"down{c}{t}", [P, HALF], F32)
+            nc.scalar.activation(high[:], h2[t][:].indirect(n4_list[:, entries]), ACT.Copy, scale=0.5)
+            nc.scalar.activation(low[:], h2[t][:].indirect(n3_list[:, entries]), ACT.Copy)
+            nc.vector.scalar_tensor_tensor(down[:], acc2[t][:, cols], -0.03125, high[:], ALU.mult, ALU.add)
+            nc.vector.scalar_tensor_tensor(up[:], acc2[t][:, cols], 0.0625, low[:], ALU.mult, ALU.subtract)
+            return c, t, up, down
+
+        def clip(c, t, up, down):
+            nc.vector.tensor_scalar(down[:], down[:], 0.0, None, ALU.max)
+
+        def finish(c, t, up, down):
+            cols = slice(c * HALF, (c + 1) * HALF)
+            nc.vector.scalar_tensor_tensor(y[c][:, t, :], up[:], 0.0, down[:], ALU.max, ALU.add)
+            if t % 2 == 1:
+                nc.sync.dma_start(out_rows[:, t - 1 : t + 1, cols], y[c][:, t - 1 : t + 1, :])
+
+        before = None
+        for c in range(2):
+            for t in range(PACK):
+                unit = differences(c, t)
+                if before is not None:
+                    finish(*before)
+                clip(*unit)
+                before = unit
+        finish(*before)
+
+        for c, copy in enumerate((nc.scalar.copy, nc.vector.tensor_copy)):
+            copy(
+                rounded[:, c * HALF : (c + 1) * HALF, :].rearrange("p (n i) t -> p n t i", i=4),
+                y[c][:].rearrange("p t (n i) -> p n t i", i=4),
+            )
+        y_words = sb("y_words", [P, S], U32)
+        y_scales = sb("y_scales", [P, S], U8)
+        nc.vector.quantize_mx(
+            out=y_words[:].bitcast(FP8X4), scales=y_scales[:], in_=rounded[:].rearrange("p n t -> p (n t)")
+        )
+        nc.sync.dma_start(out_1[0].rearrange("p n t -> p (n t)").bitcast(I32), y_words[:].bitcast(I32))
+        for q in range(4):
+            queue = nc.scalar if q % 2 == 0 else nc.sync
+            queue.dma_start(out_2[0, 4 * q : 4 * q + 4, :].bitcast(I32), y_scales[32 * q : 32 * q + 4, :].bitcast(I32))

@@ -19,6 +19,7 @@ P = 128
 PACK = 4
 HALF = S // 2
 H_WINDOW = 2 * W
+H2_WINDOW = 2 * S
 
 
 def tile_picked_codekgatehinge_none_po_kernel(
@@ -47,14 +48,14 @@ def tile_picked_codekgatehinge_none_po_kernel(
             width = rows.shape[1] // 4
             nc.scalar.dma_start(table[:].bitcast(I32), rows.bitcast(I32).unsqueeze(1).to_broadcast([16, 8, width]))
 
-        k1_list = load_list("k1_list", k1)
-        load_scale_table(d_scale_table, d_scales[0])
         offs_list = load_list("offs_list", offs)
         load_scale_table(x_scale_table, x_scales[0])
-        nc.sync.dma_start(d_word_table[:].bitcast(I32), d_words[0].rearrange("p n t -> p (n t)").bitcast(I32))
+        k1_list = load_list("k1_list", k1)
+        load_scale_table(d_scale_table, d_scales[0])
         n2_list = load_list("n2_list", n2)
-        nc.sync.dma_start(x_word_table[:].bitcast(I32), x_words[0].rearrange("p n t -> p (n t)").bitcast(I32))
         n1_list = load_list("n1_list", n1)
+        nc.sync.dma_start(d_word_table[:].bitcast(I32), d_words[0].rearrange("p n t -> p (n t)").bitcast(I32))
+        nc.sync.dma_start(x_word_table[:].bitcast(I32), x_words[0].rearrange("p n t -> p (n t)").bitcast(I32))
         k2_list = load_list("k2_list", k2)
         n3_list = load_list("n3_list", n3)
         n4_list = load_list("n4_list", n4)
@@ -62,59 +63,53 @@ def tile_picked_codekgatehinge_none_po_kernel(
         nc.gpsimd.dma_start(gain[:], gs.rearrange("(p t) o -> p (t o)", t=PACK))
 
         h = [sb(f"h{t}", [P, H_WINDOW], F32) for t in range(PACK)]
+        h2 = [sb(f"h2_{t}", [P, H2_WINDOW], F32) for t in range(PACK)]
         for t in range(PACK):
             nc.vector.memset(h[t][:, S:], 0.0)
+            nc.vector.memset(h2[t][:, S:], 0.0)
 
-        def place_rows(plane, queue):
-            for j in range(1, 4):
+        def pick(picked, table, codes, piece, pieces):
+            cols = codes.shape[1] // pieces
+            nc.vector.tensor_copy(
+                picked[:, 16 * cols * piece : 16 * cols * (piece + 1)],
+                table[:].indirect(codes[:, cols * piece : cols * (piece + 1)]),
+            )
+
+        def deal(dealt, picked):
+            nc.vector.tensor_copy(
+                dealt.rearrange("p (t m) -> p t m", t=PACK), picked.rearrange("p (m t) -> p t m", t=PACK)
+            )
+
+        def place_rows(plane, queues):
+            for j, queue in enumerate(queues, 1):
                 queue.dma_start(plane[j:P:32, :].bitcast(I32), plane[8 * j : P : 32, :].bitcast(I32))
 
-        def coded_scales(name, codes, pieces, plane, tag=None):
-            picked = sb(name + "_picked", [P, H], U8, tag)
-            cols = H // 16 // pieces
-            for i in range(pieces):
-                nc.vector.tensor_copy(
-                    picked[:, 16 * cols * i : 16 * cols * (i + 1)],
-                    d_scale_table[:].indirect(codes[:, cols * i : cols * (i + 1)]),
-                )
-            nc.vector.tensor_copy(
-                plane[:, :H].rearrange("p (t m) -> p t m", t=PACK), picked[:].rearrange("p (m t) -> p t m", t=PACK)
-            )
-
-        def coded_words(name, codes, pieces, tag=None):
-            picked = sb(name + "_picked", [P, H], U32, tag)
-            cols = H // 16 // pieces
-            for i in range(pieces):
-                nc.vector.tensor_copy(
-                    picked[:, 16 * cols * i : 16 * cols * (i + 1)],
-                    d_word_table[:].indirect(codes[:, cols * i : cols * (i + 1)]),
-                )
-            return picked
-
-        def deal_words(words, picked, first, last):
-            nc.vector.tensor_copy(
-                words[:].bitcast(I32).rearrange("p (t m) -> p t m", t=PACK)[:, first:last, :],
-                picked[:].bitcast(I32).rearrange("p (m t) -> p t m", t=PACK)[:, first:last, :],
-            )
-
-        plane1 = sb("plane1", [P, H + S], U8, "plane1")
-        coded_scales("w1_scales", k1_list, 1, plane1)
+        plane1 = sb("plane1", [P, H + S], U8)
         xq_picked = sb("xq_picked", [P, S], U8)
-        nc.vector.tensor_copy(xq_picked[:], x_scale_table[:].indirect(offs_list[:]))
+        pick(xq_picked, x_scale_table, offs_list, 0, 1)
         nc.vector.tensor_copy(plane1[:, H:].bitcast(I32), xq_picked[:].bitcast(I32))
-        place_rows(plane1, nc.scalar)
-        w1_picked = coded_words("w1_words", k1_list, 1)
-        w1_words = sb("w1_words", [P, H], U32)
-        deal_words(w1_words, w1_picked, 0, PACK)
+        w1_scales_picked = sb("w1_scales_picked", [P, H], U8)
+        pick(w1_scales_picked, d_scale_table, k1_list, 0, 1)
+        deal(plane1[:, :H], w1_scales_picked[:])
+        place_rows(plane1, (nc.scalar, nc.sync, nc.scalar))
+        w1_picked = sb("w1_picked", [P, H], U32)
+        pick(w1_picked, d_word_table, k1_list, 0, 1)
+        w1_words = [sb(f"w1_words{t}", [P, P], U32) for t in range(PACK)]
         xq_words = sb("xq_words", [P, S], U32)
-        nc.vector.tensor_copy(xq_words[:], x_word_table[:].indirect(offs_list[:]))
 
+        def deal_w1(t):
+            nc.vector.tensor_copy(w1_words[t][:].bitcast(I32), w1_picked[:].bitcast(I32)[:, t:H:PACK])
+
+        deal_w1(0)
+        pick(xq_words, x_word_table, offs_list, 0, 1)
         for t in range(PACK):
+            if t + 1 < PACK:
+                deal_w1(t + 1)
             cols = slice(t * P, (t + 1) * P)
             acc = psum.tile([P, S], F32, name=f"acc1_{t}")
             nc.tensor.matmul_mx(
                 out=acc[:],
-                lhsT=w1_words[:, cols].bitcast(FP8X4),
+                lhsT=w1_words[t][:].bitcast(FP8X4),
                 lhsT_scale=plane1[:, cols],
                 rhs=xq_words[:].bitcast(FP8X4),
                 rhs_scale=plane1[:, H:],
@@ -124,35 +119,42 @@ def tile_picked_codekgatehinge_none_po_kernel(
             nc.vector.tensor_scalar(h[t][:, :S], acc[:], 0.0625, None, ALU.mult)
 
         z = [sb(f"z{c}", [P, HALF, PACK], BF16) for c in range(2)]
+        ra = [sb(f"ra{t}", [P, W], F32) for t in range(PACK)]
 
         def fetch(t):
             gate = sb(f"gate{t}", [P, W], F32)
             old = sb(f"old{t}", [P, W], F32)
-            ra = sb(f"ra{t}", [P, W], F32)
             nc.scalar.activation(gate[:], h[t][:].indirect(n2_list[:]), ACT.Sigmoid)
             nc.scalar.activation(old[:], h[t][:].indirect(n1_list[:]), ACT.Copy)
-            nc.vector.tensor_tensor(ra[:], old[:], gate[:], ALU.mult)
-            return ra
+            nc.vector.tensor_tensor(ra[t][:], old[:], gate[:], ALU.mult)
 
-        def put(t, ra):
-            nc.scalar.activation(h[t][:].indirect(n1_list[:]), ra[:], ACT.Copy)
+        def put(t):
+            nc.scalar.activation(h[t][:].indirect(n1_list[:]), ra[t][:], ACT.Copy)
             for c in range(2):
                 nc.vector.tensor_scalar(
                     z[c][:, :, t], h[t][:, c * HALF : (c + 1) * HALF], gain[:, t : t + 1], None, ALU.mult
                 )
 
-        ras = [fetch(0)]
-        for t in range(1, PACK):
-            ras.append(fetch(t))
-            put(t - 1, ras[t - 1])
-        put(PACK - 1, ras[PACK - 1])
-
+        w2_scales_picked = sb("w2_scales_picked", [P, H], U8, "plane1")
+        w2_picked = sb("w2_picked", [P, H], U32, "xq_words")
         w2_scales = sb("w2_scales", [P, H], U8)
-        coded_scales("w2_scales", k2_list, 2, w2_scales, "plane1")
-        place_rows(w2_scales, nc.sync)
-        w2_picked = coded_words("w2_words", k2_list, 2, "w1_words")
         w2_words = sb("w2_words", [P, H], U32)
-        deal_words(w2_words, w2_picked, 0, PACK)
+
+        fetch(0)
+        pick(w2_scales_picked, d_scale_table, k2_list, 0, 2)
+        fetch(1)
+        pick(w2_scales_picked, d_scale_table, k2_list, 1, 2)
+        put(0)
+        deal(w2_scales[:], w2_scales_picked[:])
+        place_rows(w2_scales, (nc.sync, nc.sync, nc.sync))
+        fetch(2)
+        pick(w2_picked, d_word_table, k2_list, 0, 2)
+        put(1)
+        fetch(3)
+        pick(w2_picked, d_word_table, k2_list, 1, 2)
+        put(2)
+        deal(w2_words[:].bitcast(I32), w2_picked[:].bitcast(I32))
+        put(3)
 
         z_words = sb("z_words", [P, S], U32)
         z_scales = sb("z_scales", [P, S], U8)
@@ -162,71 +164,116 @@ def tile_picked_codekgatehinge_none_po_kernel(
                 out=z_words[:, cols].bitcast(FP8X4), scales=z_scales[:, cols], in_=z[c][:].rearrange("p n t -> p (n t)")
             )
 
-        h2 = [sb(f"h2_{t}", [P, S], F32) for t in range(PACK)]
         acc2 = [psum.tile([P, S], F32, name=f"acc2_{t}") for t in range(PACK)]
         for t in range(PACK):
             cols = slice(t * P, (t + 1) * P)
-            nc.tensor.matmul_mx(
-                out=acc2[t][:],
-                lhsT=w2_words[:, cols].bitcast(FP8X4),
-                lhsT_scale=w2_scales[:, cols],
-                rhs=z_words[:].bitcast(FP8X4),
-                rhs_scale=z_scales[:],
-                start=True,
-                stop=True,
-            )
-            if t == 0:
-                nc.scalar.activation(h2[t][:], acc2[t][:], ACT.Copy, scale=0.0625)
-            else:
-                nc.vector.tensor_scalar(h2[t][:], acc2[t][:], 0.0625, None, ALU.mult)
+            width = HALF if t == 0 else S
+            for first in range(0, S, width):
+                places = slice(first, first + width)
+                nc.tensor.matmul_mx(
+                    out=acc2[t][:, places],
+                    lhsT=w2_words[:, cols].bitcast(FP8X4),
+                    lhsT_scale=w2_scales[:, cols],
+                    rhs=z_words[:, places].bitcast(FP8X4),
+                    rhs_scale=z_scales[:, places],
+                    start=True,
+                    stop=True,
+                )
 
         out_rows = out_0.rearrange("(p t) s -> p t s", t=PACK)
         y = [sb(f"y{c}", [P, PACK, HALF], F32) for c in range(2)]
-        rounded = sb("rounded", [P, S, PACK], BF16)
+        rounded = [sb(f"rounded{c}", [P, HALF, PACK], BF16) for c in range(2)]
+        rise = [sb(f"rise{t}", [P, S], F32) for t in range(PACK)]
+        drop = [[sb(f"drop{c}{t}", [P, HALF], F32) for t in range(PACK)] for c in range(2)]
 
-        def differences(c, t):
-            cols = slice(c * HALF, (c + 1) * HALF)
+        def empty(t):
+            nc.vector.tensor_scalar(h2[t][:, :S], acc2[t][:], 0.0625, None, ALU.mult)
+
+        def make_rise(t):
+            high = sb(f"high{t}", [P, S], F32)
+            nc.scalar.activation(high[:], h2[t][:].indirect(n4_list[:]), ACT.Copy, scale=0.5)
+            nc.vector.scalar_tensor_tensor(rise[t][:], acc2[t][:], -0.03125, high[:], ALU.mult, ALU.add)
+
+        def clip_rise(t):
+            nc.vector.tensor_scalar(rise[t][:], rise[t][:], 0.0, None, ALU.max)
+
+        low = [[sb(f"low{c}{t}", [P, HALF], F32) for t in range(PACK)] for c in range(2)]
+
+        def fetch_low(c, t):
             entries = slice(c * HALF // 16, (c + 1) * HALF // 16)
-            low = sb(f"low{c}{t}", [P, HALF], F32)
-            high = sb(f"high{c}{t}", [P, HALF], F32)
-            up = sb(f"up{c}{t}", [P, HALF], F32)
-            down = sb(f"down{c}{t}", [P, HALF], F32)
-            nc.scalar.activation(high[:], h2[t][:].indirect(n4_list[:, entries]), ACT.Copy, scale=0.5)
-            nc.scalar.activation(low[:], h2[t][:].indirect(n3_list[:, entries]), ACT.Copy)
-            nc.vector.scalar_tensor_tensor(down[:], acc2[t][:, cols], -0.03125, high[:], ALU.mult, ALU.add)
-            nc.vector.scalar_tensor_tensor(up[:], acc2[t][:, cols], 0.0625, low[:], ALU.mult, ALU.subtract)
-            return c, t, up, down
+            nc.scalar.activation(low[c][t][:], h2[t][:].indirect(n3_list[:, entries]), ACT.Copy)
 
-        def clip(c, t, up, down):
-            nc.vector.tensor_scalar(down[:], down[:], 0.0, None, ALU.max)
-
-        def finish(c, t, up, down):
-            cols = slice(c * HALF, (c + 1) * HALF)
-            nc.vector.scalar_tensor_tensor(y[c][:, t, :], up[:], 0.0, down[:], ALU.max, ALU.add)
-            if t % 2 == 1:
-                nc.sync.dma_start(out_rows[:, t - 1 : t + 1, cols], y[c][:, t - 1 : t + 1, :])
-
-        before = None
-        for c in range(2):
-            for t in range(PACK):
-                unit = differences(c, t)
-                if before is not None:
-                    finish(*before)
-                clip(*unit)
-                before = unit
-        finish(*before)
-
-        for c, copy in enumerate((nc.scalar.copy, nc.vector.tensor_copy)):
-            copy(
-                rounded[:, c * HALF : (c + 1) * HALF, :].rearrange("p (n i) t -> p n t i", i=4),
-                y[c][:].rearrange("p t (n i) -> p n t i", i=4),
+        def make_drop(c, t, part=slice(0, HALF)):
+            cols = slice(c * HALF + part.start, c * HALF + part.stop)
+            nc.vector.scalar_tensor_tensor(
+                drop[c][t][:, part], acc2[t][:, cols], 0.0625, low[c][t][:, part], ALU.mult, ALU.subtract
             )
+
+        def finish(c, t, part=slice(0, HALF)):
+            cols = slice(c * HALF + part.start, c * HALF + part.stop)
+            nc.vector.scalar_tensor_tensor(
+                y[c][:, t, part], drop[c][t][:, part], 0.0, rise[t][:, cols], ALU.max, ALU.add
+            )
+
+        def store(c, t):
+            nc.sync.dma_start(out_rows[:, t : t + 2, c * HALF : (c + 1) * HALF], y[c][:, t : t + 2, :])
+
         y_words = sb("y_words", [P, S], U32)
         y_scales = sb("y_scales", [P, S], U8)
-        nc.vector.quantize_mx(
-            out=y_words[:].bitcast(FP8X4), scales=y_scales[:], in_=rounded[:].rearrange("p n t -> p (n t)")
-        )
-        nc.sync.dma_start(out_1[0].rearrange("p n t -> p (n t)").bitcast(I32), y_words[:].bitcast(I32))
+        out_words = out_1[0].rearrange("p n t -> p (n t)").bitcast(I32)
+
+        def round_y(copy, c, part):
+            copy(
+                rounded[c][:, part, :].rearrange("p (n i) t -> p n t i", i=4),
+                y[c][:, :, part].rearrange("p t (n i) -> p n t i", i=4),
+            )
+
+        def quantize_y(c, part):
+            cols = slice(c * HALF + part.start, c * HALF + part.stop)
+            nc.vector.quantize_mx(
+                out=y_words[:, cols].bitcast(FP8X4),
+                scales=y_scales[:, cols],
+                in_=rounded[c][:, part, :].rearrange("p n t -> p (n t)"),
+            )
+
+        nc.scalar.activation(h2[0][:, :S], acc2[0][:], ACT.Copy, scale=0.0625)
+        for t in range(1, PACK):
+            empty(t)
+        for t in range(PACK):
+            make_rise(t)
+            if t > 0:
+                finish(0, t - 1)
+            fetch_low(0, t)
+            make_drop(0, t)
+            clip_rise(t)
+        store(0, 0)
+        last = PACK - 1
+        for t in range(last):
+            fetch_low(1, t)
+            make_drop(1, t)
+            if t == 0:
+                finish(0, last)
+                store(0, 2)
+            else:
+                finish(1, t - 1)
+        fetch_low(1, last)
+        whole = slice(0, HALF)
+        parts = (slice(0, HALF // 2), slice(HALF // 2, HALF))
+        round_y(nc.scalar.copy, 0, whole)
+        finish(1, last - 1)
+        store(1, 0)
+        for part in parts:
+            make_drop(1, last, part)
+        for part in parts:
+            finish(1, last, part)
+        store(1, 2)
+        quantize_y(0, whole)
+        nc.sync.dma_start(out_words[:, :HALF], y_words[:, :HALF].bitcast(I32))
+        for part in parts:
+            round_y(nc.vector.tensor_copy, 1, part)
+        for part in parts:
+            quantize_y(1, part)
+        nc.sync.dma_start(out_words[:, HALF:], y_words[:, HALF:].bitcast(I32))
         for q in range(4):
             queue = nc.scalar if q % 2 == 0 else nc.sync
             queue.dma_start(out_2[0, 4 * q : 4 * q + 4, :].bitcast(I32), y_scales[32 * q : 32 * q + 4, :].bitcast(I32))

@@ -54,8 +54,8 @@ def tile_picked_codekgatehinge_none_po_kernel(
         load_scale_table(d_scale_table, d_scales[0])
         n2_list = load_list("n2_list", n2)
         n1_list = load_list("n1_list", n1)
-        nc.sync.dma_start(d_word_table[:].bitcast(I32), d_words[0].rearrange("p n t -> p (n t)").bitcast(I32))
-        nc.sync.dma_start(x_word_table[:].bitcast(I32), x_words[0].rearrange("p n t -> p (n t)").bitcast(I32))
+        nc.scalar.dma_start(d_word_table[:].bitcast(I32), d_words[0].rearrange("p n t -> p (n t)").bitcast(I32))
+        nc.scalar.dma_start(x_word_table[:].bitcast(I32), x_words[0].rearrange("p n t -> p (n t)").bitcast(I32))
         k2_list = load_list("k2_list", k2)
         n3_list = load_list("n3_list", n3)
         n4_list = load_list("n4_list", n4)
@@ -91,7 +91,7 @@ def tile_picked_codekgatehinge_none_po_kernel(
         w1_scales_picked = sb("w1_scales_picked", [P, H], U8)
         pick(w1_scales_picked, d_scale_table, k1_list, 0, 1)
         deal(plane1[:, :H], w1_scales_picked[:])
-        place_rows(plane1, (nc.scalar, nc.sync, nc.scalar))
+        place_rows(plane1, (nc.sync, nc.sync, nc.sync))
         w1_picked = sb("w1_picked", [P, H], U32)
         pick(w1_picked, d_word_table, k1_list, 0, 1)
         w1_words = [sb(f"w1_words{t}", [P, P], U32) for t in range(PACK)]
@@ -135,12 +135,11 @@ def tile_picked_codekgatehinge_none_po_kernel(
                     z[c][:, :, t], h[t][:, c * HALF : (c + 1) * HALF], gain[:, t : t + 1], None, ALU.mult
                 )
 
-        w2_scales_picked = sb("w2_scales_picked", [P, H], U8, "plane1")
-        w2_picked = sb("w2_picked", [P, H], U32, "xq_words")
         w2_scales = sb("w2_scales", [P, H], U8)
         w2_words = sb("w2_words", [P, H], U32)
 
         fetch(0)
+        w2_scales_picked = sb("w2_scales_picked", [P, H], U8, "gate0")
         pick(w2_scales_picked, d_scale_table, k2_list, 0, 2)
         fetch(1)
         pick(w2_scales_picked, d_scale_table, k2_list, 1, 2)
@@ -148,6 +147,7 @@ def tile_picked_codekgatehinge_none_po_kernel(
         deal(w2_scales[:], w2_scales_picked[:])
         place_rows(w2_scales, (nc.sync, nc.sync, nc.sync))
         fetch(2)
+        w2_picked = sb("w2_picked", [P, H], U32, "gate1")
         pick(w2_picked, d_word_table, k2_list, 0, 2)
         put(1)
         fetch(3)
@@ -268,12 +268,11 @@ def tile_picked_codekgatehinge_none_po_kernel(
             finish(1, last, part)
         store(1, 2)
         quantize_y(0, whole)
-        nc.sync.dma_start(out_words[:, :HALF], y_words[:, :HALF].bitcast(I32))
         for part in parts:
             round_y(nc.vector.tensor_copy, 1, part)
         for part in parts:
             quantize_y(1, part)
-        nc.sync.dma_start(out_words[:, HALF:], y_words[:, HALF:].bitcast(I32))
+        nc.sync.dma_start(out_words, y_words[:].bitcast(I32))
         for q in range(4):
             queue = nc.scalar if q % 2 == 0 else nc.sync
             queue.dma_start(out_2[0, 4 * q : 4 * q + 4, :].bitcast(I32), y_scales[32 * q : 32 * q + 4, :].bitcast(I32))

@@ -17,9 +17,14 @@ ACT = mybir.ActivationFunctionType
 
 P = 128
 PACK = 4
+GROUP = 16
+QUADRANT = 32
+BLOCK_PARTITIONS = 8
+SCALE_ROWS = P // BLOCK_PARTITIONS
 HALF = S // 2
 H_WINDOW = 2 * W
 H2_WINDOW = 2 * S
+SIXTEENTH = 0.0625
 
 
 def tile_picked_codekgatehinge_none_po_kernel(
@@ -32,9 +37,9 @@ def tile_picked_codekgatehinge_none_po_kernel(
         psum = ctx.enter_context(tc.psum_pool(name="psum", bufs=1))
 
         def load_list(name, src):
-            t = lists.tile([P, src.shape[1]], U16, name=name)
-            nc.sync.dma_start(t[:], src)
-            return t
+            entries = lists.tile([P, src.shape[1]], U16, name=name)
+            nc.sync.dma_start(entries[:], src)
+            return entries
 
         def sb(name, shape, dtype, tag=None):
             return keep.tile(shape, dtype, name=name, tag=tag or name, align_bytes=64)
@@ -45,8 +50,9 @@ def tile_picked_codekgatehinge_none_po_kernel(
         x_word_table = sb("x_word_table", [P, T], U32)
 
         def load_scale_table(table, rows):
-            width = rows.shape[1] // 4
-            nc.scalar.dma_start(table[:].bitcast(I32), rows.bitcast(I32).unsqueeze(1).to_broadcast([16, 8, width]))
+            as_int32 = rows.bitcast(I32)
+            spread = as_int32.unsqueeze(1).to_broadcast([SCALE_ROWS, BLOCK_PARTITIONS, as_int32.shape[1]])
+            nc.scalar.dma_start(table[:].bitcast(I32), spread)
 
         offs_list = load_list("offs_list", offs)
         load_scale_table(x_scale_table, x_scales[0])
@@ -68,11 +74,11 @@ def tile_picked_codekgatehinge_none_po_kernel(
             nc.vector.memset(h[t][:, S:], 0.0)
             nc.vector.memset(h2[t][:, S:], 0.0)
 
-        def pick(picked, table, codes, piece, pieces):
-            cols = codes.shape[1] // pieces
+        def pick(picked, table, entries, piece, pieces):
+            cols = entries.shape[1] // pieces
             nc.vector.tensor_copy(
-                picked[:, 16 * cols * piece : 16 * cols * (piece + 1)],
-                table[:].indirect(codes[:, cols * piece : cols * (piece + 1)]),
+                picked[:, GROUP * cols * piece : GROUP * cols * (piece + 1)],
+                table[:].indirect(entries[:, cols * piece : cols * (piece + 1)]),
             )
 
         def deal(dealt, picked):
@@ -80,9 +86,11 @@ def tile_picked_codekgatehinge_none_po_kernel(
                 dealt.rearrange("p (t m) -> p t m", t=PACK), picked.rearrange("p (m t) -> p t m", t=PACK)
             )
 
-        def place_rows(plane, queues):
-            for j, queue in enumerate(queues, 1):
-                queue.dma_start(plane[j:P:32, :].bitcast(I32), plane[8 * j : P : 32, :].bitcast(I32))
+        def place_rows(plane):
+            for j in range(1, QUADRANT // BLOCK_PARTITIONS):
+                nc.sync.dma_start(
+                    plane[j:P:QUADRANT, :].bitcast(I32), plane[BLOCK_PARTITIONS * j : P : QUADRANT, :].bitcast(I32)
+                )
 
         plane1 = sb("plane1", [P, H + S], U8)
         xq_picked = sb("xq_picked", [P, S], U8)
@@ -91,7 +99,7 @@ def tile_picked_codekgatehinge_none_po_kernel(
         w1_scales_picked = sb("w1_scales_picked", [P, H], U8)
         pick(w1_scales_picked, d_scale_table, k1_list, 0, 1)
         deal(plane1[:, :H], w1_scales_picked[:])
-        place_rows(plane1, (nc.sync, nc.sync, nc.sync))
+        place_rows(plane1)
         w1_picked = sb("w1_picked", [P, H], U32)
         pick(w1_picked, d_word_table, k1_list, 0, 1)
         w1_words = [sb(f"w1_words{t}", [P, P], U32) for t in range(PACK)]
@@ -100,23 +108,35 @@ def tile_picked_codekgatehinge_none_po_kernel(
         def deal_w1(t):
             nc.vector.tensor_copy(w1_words[t][:].bitcast(I32), w1_picked[:].bitcast(I32)[:, t:H:PACK])
 
-        deal_w1(0)
-        pick(xq_words, x_word_table, offs_list, 0, 1)
-        for t in range(PACK):
-            if t + 1 < PACK:
-                deal_w1(t + 1)
-            cols = slice(t * P, (t + 1) * P)
-            acc = psum.tile([P, S], F32, name=f"acc1_{t}")
+        def product(bank, weights, weight_scales, words, scales, places):
+            acc = psum.tile([P, places.stop - places.start], F32, name=bank, tag=bank)
             nc.tensor.matmul_mx(
                 out=acc[:],
-                lhsT=w1_words[t][:].bitcast(FP8X4),
-                lhsT_scale=plane1[:, cols],
-                rhs=xq_words[:].bitcast(FP8X4),
-                rhs_scale=plane1[:, H:],
+                lhsT=weights.bitcast(FP8X4),
+                lhsT_scale=weight_scales,
+                rhs=words[:, places].bitcast(FP8X4),
+                rhs_scale=scales[:, places],
                 start=True,
                 stop=True,
             )
-            nc.vector.tensor_scalar(h[t][:, :S], acc[:], 0.0625, None, ALU.mult)
+            return acc
+
+        halves = [slice(c * HALF, (c + 1) * HALF) for c in range(2)]
+
+        def first_layer(bank, t, places):
+            acc = product(bank, w1_words[t][:], plane1[:, t * P : (t + 1) * P], xq_words, plane1[:, H:], places)
+            nc.vector.tensor_scalar(h[t][:, places], acc[:], SIXTEENTH, None, ALU.mult)
+
+        deal_w1(0)
+        for c in range(2):
+            pick(xq_words, x_word_table, offs_list, c, 2)
+        first_layer("bank0", 0, halves[0])
+        deal_w1(1)
+        first_layer("bank1", 0, halves[1])
+        for t in range(1, PACK):
+            if t + 1 < PACK:
+                deal_w1(t + 1)
+            first_layer(f"bank{t + 1}", t, slice(0, S))
 
         z = [sb(f"z{c}", [P, HALF, PACK], BF16) for c in range(2)]
         ra = [sb(f"ra{t}", [P, W], F32) for t in range(PACK)]
@@ -132,7 +152,7 @@ def tile_picked_codekgatehinge_none_po_kernel(
             nc.scalar.activation(h[t][:].indirect(n1_list[:]), ra[t][:], ACT.Copy)
             for c in range(2):
                 nc.vector.tensor_scalar(
-                    z[c][:, :, t], h[t][:, c * HALF : (c + 1) * HALF], gain[:, t : t + 1], None, ALU.mult
+                    z[c][:, :, t], h[t][:, halves[c]], gain[:, t : t + 1], None, ALU.mult
                 )
 
         w2_scales = sb("w2_scales", [P, H], U8)
@@ -145,7 +165,7 @@ def tile_picked_codekgatehinge_none_po_kernel(
         pick(w2_scales_picked, d_scale_table, k2_list, 1, 2)
         put(0)
         deal(w2_scales[:], w2_scales_picked[:])
-        place_rows(w2_scales, (nc.sync, nc.sync, nc.sync))
+        place_rows(w2_scales)
         fetch(2)
         w2_picked = sb("w2_picked", [P, H], U32, "gate1")
         pick(w2_picked, d_word_table, k2_list, 0, 2)
@@ -159,26 +179,21 @@ def tile_picked_codekgatehinge_none_po_kernel(
         z_words = sb("z_words", [P, S], U32)
         z_scales = sb("z_scales", [P, S], U8)
         for c in range(2):
-            cols = slice(c * HALF, (c + 1) * HALF)
             nc.vector.quantize_mx(
-                out=z_words[:, cols].bitcast(FP8X4), scales=z_scales[:, cols], in_=z[c][:].rearrange("p n t -> p (n t)")
+                out=z_words[:, halves[c]].bitcast(FP8X4),
+                scales=z_scales[:, halves[c]],
+                in_=z[c][:].rearrange("p n t -> p (n t)"),
             )
 
-        acc2 = [psum.tile([P, S], F32, name=f"acc2_{t}") for t in range(PACK)]
-        for t in range(PACK):
+        def second_layer(bank, t, places):
             cols = slice(t * P, (t + 1) * P)
-            width = HALF if t == 0 else S
-            for first in range(0, S, width):
-                places = slice(first, first + width)
-                nc.tensor.matmul_mx(
-                    out=acc2[t][:, places],
-                    lhsT=w2_words[:, cols].bitcast(FP8X4),
-                    lhsT_scale=w2_scales[:, cols],
-                    rhs=z_words[:, places].bitcast(FP8X4),
-                    rhs_scale=z_scales[:, places],
-                    start=True,
-                    stop=True,
-                )
+            return product(bank, w2_words[:, cols], w2_scales[:, cols], z_words, z_scales, places)
+
+        acc2 = [[second_layer(f"bank{c}", 0, halves[c])[:] for c in range(2)]]
+        wide = [None]
+        for t in range(1, PACK):
+            wide.append(second_layer(f"bank{t + 1}", t, slice(0, S)))
+            acc2.append([wide[t][:, halves[c]] for c in range(2)])
 
         out_rows = out_0.rearrange("(p t) s -> p t s", t=PACK)
         y = [sb(f"y{c}", [P, PACK, HALF], F32) for c in range(2)]
@@ -187,12 +202,18 @@ def tile_picked_codekgatehinge_none_po_kernel(
         drop = [[sb(f"drop{c}{t}", [P, HALF], F32) for t in range(PACK)] for c in range(2)]
 
         def empty(t):
-            nc.vector.tensor_scalar(h2[t][:, :S], acc2[t][:], 0.0625, None, ALU.mult)
+            nc.vector.tensor_scalar(h2[t][:, :S], wide[t][:], SIXTEENTH, None, ALU.mult)
 
         def make_rise(t):
             high = sb(f"high{t}", [P, S], F32)
             nc.scalar.activation(high[:], h2[t][:].indirect(n4_list[:]), ACT.Copy, scale=0.5)
-            nc.vector.scalar_tensor_tensor(rise[t][:], acc2[t][:], -0.03125, high[:], ALU.mult, ALU.add)
+            if t == 0:
+                for c in range(2):
+                    nc.vector.scalar_tensor_tensor(
+                        rise[t][:, halves[c]], acc2[t][c], -SIXTEENTH / 2, high[:, halves[c]], ALU.mult, ALU.add
+                    )
+            else:
+                nc.vector.scalar_tensor_tensor(rise[t][:], wide[t][:], -SIXTEENTH / 2, high[:], ALU.mult, ALU.add)
 
         def clip_rise(t):
             nc.vector.tensor_scalar(rise[t][:], rise[t][:], 0.0, None, ALU.max)
@@ -200,23 +221,24 @@ def tile_picked_codekgatehinge_none_po_kernel(
         low = [[sb(f"low{c}{t}", [P, HALF], F32) for t in range(PACK)] for c in range(2)]
 
         def fetch_low(c, t):
-            entries = slice(c * HALF // 16, (c + 1) * HALF // 16)
-            nc.scalar.activation(low[c][t][:], h2[t][:].indirect(n3_list[:, entries]), ACT.Copy)
+            list_cols = slice(c * HALF // GROUP, (c + 1) * HALF // GROUP)
+            nc.scalar.activation(low[c][t][:], h2[t][:].indirect(n3_list[:, list_cols]), ACT.Copy)
 
-        def make_drop(c, t, part=slice(0, HALF)):
-            cols = slice(c * HALF + part.start, c * HALF + part.stop)
+        whole = slice(0, HALF)
+
+        def make_drop(c, t, part=whole):
             nc.vector.scalar_tensor_tensor(
-                drop[c][t][:, part], acc2[t][:, cols], 0.0625, low[c][t][:, part], ALU.mult, ALU.subtract
+                drop[c][t][:, part], acc2[t][c][:, part], SIXTEENTH, low[c][t][:, part], ALU.mult, ALU.subtract
             )
 
-        def finish(c, t, part=slice(0, HALF)):
+        def finish(c, t, part=whole):
             cols = slice(c * HALF + part.start, c * HALF + part.stop)
             nc.vector.scalar_tensor_tensor(
                 y[c][:, t, part], drop[c][t][:, part], 0.0, rise[t][:, cols], ALU.max, ALU.add
             )
 
         def store(c, t):
-            nc.sync.dma_start(out_rows[:, t : t + 2, c * HALF : (c + 1) * HALF], y[c][:, t : t + 2, :])
+            nc.sync.dma_start(out_rows[:, t : t + 2, halves[c]], y[c][:, t : t + 2, :])
 
         y_words = sb("y_words", [P, S], U32)
         y_scales = sb("y_scales", [P, S], U8)
@@ -228,15 +250,8 @@ def tile_picked_codekgatehinge_none_po_kernel(
                 y[c][:, :, part].rearrange("p t (n i) -> p n t i", i=4),
             )
 
-        def quantize_y(c, part):
-            cols = slice(c * HALF + part.start, c * HALF + part.stop)
-            nc.vector.quantize_mx(
-                out=y_words[:, cols].bitcast(FP8X4),
-                scales=y_scales[:, cols],
-                in_=rounded[c][:, part, :].rearrange("p n t -> p (n t)"),
-            )
-
-        nc.scalar.activation(h2[0][:, :S], acc2[0][:], ACT.Copy, scale=0.0625)
+        for c in range(2):
+            nc.scalar.activation(h2[0][:, halves[c]], acc2[0][c], ACT.Copy, scale=SIXTEENTH)
         for t in range(1, PACK):
             empty(t)
         for t in range(PACK):
@@ -257,7 +272,6 @@ def tile_picked_codekgatehinge_none_po_kernel(
             else:
                 finish(1, t - 1)
         fetch_low(1, last)
-        whole = slice(0, HALF)
         parts = (slice(0, HALF // 2), slice(HALF // 2, HALF))
         round_y(nc.scalar.copy, 0, whole)
         finish(1, last - 1)
@@ -267,12 +281,19 @@ def tile_picked_codekgatehinge_none_po_kernel(
         for part in parts:
             finish(1, last, part)
         store(1, 2)
-        quantize_y(0, whole)
         for part in parts:
             round_y(nc.vector.tensor_copy, 1, part)
-        for part in parts:
-            quantize_y(1, part)
+        for c in range(2):
+            nc.vector.quantize_mx(
+                out=y_words[:, halves[c]].bitcast(FP8X4),
+                scales=y_scales[:, halves[c]],
+                in_=rounded[c][:].rearrange("p n t -> p (n t)"),
+            )
         nc.sync.dma_start(out_words, y_words[:].bitcast(I32))
-        for q in range(4):
+        rows = QUADRANT // BLOCK_PARTITIONS
+        for q in range(P // QUADRANT):
             queue = nc.scalar if q % 2 == 0 else nc.sync
-            queue.dma_start(out_2[0, 4 * q : 4 * q + 4, :].bitcast(I32), y_scales[32 * q : 32 * q + 4, :].bitcast(I32))
+            queue.dma_start(
+                out_2[0, rows * q : rows * (q + 1), :].bitcast(I32),
+                y_scales[QUADRANT * q : QUADRANT * q + rows, :].bitcast(I32),
+            )

from contextlib import ExitStack

import concourse.mybir as mybir

K, T, S, G, H, W = 512, 1024, 256, 2048, 512, 192
FLOPS = 2 * 2 * K * H * S

F32 = mybir.dt.float32
BF16 = mybir.dt.bfloat16
I32 = mybir.dt.int32
U32 = mybir.dt.uint32
U16 = mybir.dt.uint16
U8 = mybir.dt.uint8
FP8X4 = mybir.dt.float8_e4m3fn_x4
ALU = mybir.AluOpType
ACT = mybir.ActivationFunctionType

P = 128
PACK = 4
GROUP = 16
QUADRANT = 32
BLOCK_PARTITIONS = 8
SCALE_ROWS = P // BLOCK_PARTITIONS
HALF = S // 2
H_WINDOW = 2 * W
H2_WINDOW = 2 * S
SIXTEENTH = 0.0625


def tile_picked_codekgatehinge_none_po_kernel(
    tc, x_words, x_scales, d_words, d_scales, gs, offs, k1, n1, n2, k2, n3, n4, out_0, out_1, out_2
):
    nc = tc.nc
    with ExitStack() as ctx:
        lists = ctx.enter_context(tc.tile_pool(name="lists", bufs=1))
        keep = ctx.enter_context(tc.tile_pool(name="keep", bufs=1))
        psum = ctx.enter_context(tc.psum_pool(name="psum", bufs=1))

        def load_list(name, src):
            entries = lists.tile([P, src.shape[1]], U16, name=name)
            nc.sync.dma_start(entries[:], src)
            return entries

        def sb(name, shape, dtype, tag=None):
            return keep.tile(shape, dtype, name=name, tag=tag or name, align_bytes=64)

        d_scale_table = sb("d_scale_table", [P, G], U8)
        x_scale_table = sb("x_scale_table", [P, T], U8)
        d_word_table = sb("d_word_table", [P, G], U32)
        x_word_table = sb("x_word_table", [P, T], U32)

        def load_scale_table(table, rows):
            as_int32 = rows.bitcast(I32)
            spread = as_int32.unsqueeze(1).to_broadcast([SCALE_ROWS, BLOCK_PARTITIONS, as_int32.shape[1]])
            nc.scalar.dma_start(table[:].bitcast(I32), spread)

        offs_list = load_list("offs_list", offs)
        load_scale_table(x_scale_table, x_scales[0])
        k1_list = load_list("k1_list", k1)
        load_scale_table(d_scale_table, d_scales[0])
        n2_list = load_list("n2_list", n2)
        n1_list = load_list("n1_list", n1)
        nc.scalar.dma_start(d_word_table[:].bitcast(I32), d_words[0].rearrange("p n t -> p (n t)").bitcast(I32))
        nc.scalar.dma_start(x_word_table[:].bitcast(I32), x_words[0].rearrange("p n t -> p (n t)").bitcast(I32))
        k2_list = load_list("k2_list", k2)
        n3_list = load_list("n3_list", n3)
        n4_list = load_list("n4_list", n4)
        gain = sb("gain", [P, PACK], F32)
        nc.gpsimd.dma_start(gain[:], gs.rearrange("(p t) o -> p (t o)", t=PACK))

        h = [sb(f"h{t}", [P, H_WINDOW], F32) for t in range(PACK)]
        h2 = [sb(f"h2_{t}", [P, H2_WINDOW], F32) for t in range(PACK)]
        for t in range(PACK):
            nc.vector.memset(h[t][:, S:], 0.0)
            nc.vector.memset(h2[t][:, S:], 0.0)

        def pick(picked, table, entries, piece, pieces):
            cols = entries.shape[1] // pieces
            nc.vector.tensor_copy(
                picked[:, GROUP * cols * piece : GROUP * cols * (piece + 1)],
                table[:].indirect(entries[:, cols * piece : cols * (piece + 1)]),
            )

        def deal(dealt, picked):
            nc.vector.tensor_copy(
                dealt.rearrange("p (t m) -> p t m", t=PACK), picked.rearrange("p (m t) -> p t m", t=PACK)
            )

        def place_rows(plane):
            for j in range(1, QUADRANT // BLOCK_PARTITIONS):
                nc.sync.dma_start(
                    plane[j:P:QUADRANT, :].bitcast(I32), plane[BLOCK_PARTITIONS * j : P : QUADRANT, :].bitcast(I32)
                )

        plane1 = sb("plane1", [P, H + S], U8)
        xq_picked = sb("xq_picked", [P, S], U8)
        pick(xq_picked, x_scale_table, offs_list, 0, 1)
        nc.vector.tensor_copy(plane1[:, H:].bitcast(I32), xq_picked[:].bitcast(I32))
        w1_scales_picked = sb("w1_scales_picked", [P, H], U8)
        pick(w1_scales_picked, d_scale_table, k1_list, 0, 1)
        deal(plane1[:, :H], w1_scales_picked[:])
        place_rows(plane1)
        w1_picked = sb("w1_picked", [P, H], U32)
        pick(w1_picked, d_word_table, k1_list, 0, 1)
        w1_words = [sb(f"w1_words{t}", [P, P], U32) for t in range(PACK)]
        xq_words = sb("xq_words", [P, S], U32)

        def deal_w1(t):
            nc.vector.tensor_copy(w1_words[t][:].bitcast(I32), w1_picked[:].bitcast(I32)[:, t:H:PACK])

        def product(bank, weights, weight_scales, words, scales, places):
            acc = psum.tile([P, places.stop - places.start], F32, name=bank, tag=bank)
            nc.tensor.matmul_mx(
                out=acc[:],
                lhsT=weights.bitcast(FP8X4),
                lhsT_scale=weight_scales,
                rhs=words[:, places].bitcast(FP8X4),
                rhs_scale=scales[:, places],
                start=True,
                stop=True,
            )
            return acc

        halves = [slice(c * HALF, (c + 1) * HALF) for c in range(2)]

        def first_layer(bank, t, places):
            acc = product(bank, w1_words[t][:], plane1[:, t * P : (t + 1) * P], xq_words, plane1[:, H:], places)
            nc.vector.tensor_scalar(h[t][:, places], acc[:], SIXTEENTH, None, ALU.mult)

        deal_w1(0)
        for c in range(2):
            pick(xq_words, x_word_table, offs_list, c, 2)
        first_layer("bank0", 0, halves[0])
        deal_w1(1)
        first_layer("bank1", 0, halves[1])
        for t in range(1, PACK):
            if t + 1 < PACK:
                deal_w1(t + 1)
            first_layer(f"bank{t + 1}", t, slice(0, S))

        z = [sb(f"z{c}", [P, HALF, PACK], BF16) for c in range(2)]
        ra = [sb(f"ra{t}", [P, W], F32) for t in range(PACK)]

        def fetch(t):
            gate = sb(f"gate{t}", [P, W], F32)
            old = sb(f"old{t}", [P, W], F32)
            nc.scalar.activation(gate[:], h[t][:].indirect(n2_list[:]), ACT.Sigmoid)
            nc.scalar.activation(old[:], h[t][:].indirect(n1_list[:]), ACT.Copy)
            nc.vector.tensor_tensor(ra[t][:], old[:], gate[:], ALU.mult)

        def put(t):
            nc.scalar.activation(h[t][:].indirect(n1_list[:]), ra[t][:], ACT.Copy)
            for c in range(2):
                nc.vector.tensor_scalar(
                    z[c][:, :, t], h[t][:, halves[c]], gain[:, t : t + 1], None, ALU.mult
                )

        w2_scales = sb("w2_scales", [P, H], U8)
        w2_words = sb("w2_words", [P, H], U32)

        fetch(0)
        w2_scales_picked = sb("w2_scales_picked", [P, H], U8, "gate0")
        pick(w2_scales_picked, d_scale_table, k2_list, 0, 2)
        fetch(1)
        pick(w2_scales_picked, d_scale_table, k2_list, 1, 2)
        put(0)
        deal(w2_scales[:], w2_scales_picked[:])
        place_rows(w2_scales)
        fetch(2)
        w2_picked = sb("w2_picked", [P, H], U32, "gate1")
        pick(w2_picked, d_word_table, k2_list, 0, 2)
        put(1)
        fetch(3)
        pick(w2_picked, d_word_table, k2_list, 1, 2)
        put(2)
        deal(w2_words[:].bitcast(I32), w2_picked[:].bitcast(I32))
        put(3)

        z_words = sb("z_words", [P, S], U32)
        z_scales = sb("z_scales", [P, S], U8)
        for c in range(2):
            nc.vector.quantize_mx(
                out=z_words[:, halves[c]].bitcast(FP8X4),
                scales=z_scales[:, halves[c]],
                in_=z[c][:].rearrange("p n t -> p (n t)"),
            )

        def second_layer(bank, t, places):
            cols = slice(t * P, (t + 1) * P)
            return product(bank, w2_words[:, cols], w2_scales[:, cols], z_words, z_scales, places)

        acc2 = [[second_layer(f"bank{c}", 0, halves[c])[:] for c in range(2)]]
        wide = [None]
        for t in range(1, PACK):
            wide.append(second_layer(f"bank{t + 1}", t, slice(0, S)))
            acc2.append([wide[t][:, halves[c]] for c in range(2)])

        out_rows = out_0.rearrange("(p t) s -> p t s", t=PACK)
        y = [sb(f"y{c}", [P, PACK, HALF], F32) for c in range(2)]
        rounded = [sb(f"rounded{c}", [P, HALF, PACK], BF16) for c in range(2)]
        rise = [sb(f"rise{t}", [P, S], F32) for t in range(PACK)]
        drop = [[sb(f"drop{c}{t}", [P, HALF], F32) for t in range(PACK)] for c in range(2)]

        def empty(t):
            nc.vector.tensor_scalar(h2[t][:, :S], wide[t][:], SIXTEENTH, None, ALU.mult)

        def make_rise(t):
            high = sb(f"high{t}", [P, S], F32)
            nc.scalar.activation(high[:], h2[t][:].indirect(n4_list[:]), ACT.Copy, scale=0.5)
            if t == 0:
                for c in range(2):
                    nc.vector.scalar_tensor_tensor(
                        rise[t][:, halves[c]], acc2[t][c], -SIXTEENTH / 2, high[:, halves[c]], ALU.mult, ALU.add
                    )
            else:
                nc.vector.scalar_tensor_tensor(rise[t][:], wide[t][:], -SIXTEENTH / 2, high[:], ALU.mult, ALU.add)

        def clip_rise(t):
            nc.vector.tensor_scalar(rise[t][:], rise[t][:], 0.0, None, ALU.max)

        low = [[sb(f"low{c}{t}", [P, HALF], F32) for t in range(PACK)] for c in range(2)]

        def fetch_low(c, t):
            list_cols = slice(c * HALF // GROUP, (c + 1) * HALF // GROUP)
            nc.scalar.activation(low[c][t][:], h2[t][:].indirect(n3_list[:, list_cols]), ACT.Copy)

        whole = slice(0, HALF)

        def make_drop(c, t, part=whole):
            nc.vector.scalar_tensor_tensor(
                drop[c][t][:, part], acc2[t][c][:, part], SIXTEENTH, low[c][t][:, part], ALU.mult, ALU.subtract
            )

        def finish(c, t, part=whole):
            cols = slice(c * HALF + part.start, c * HALF + part.stop)
            nc.vector.scalar_tensor_tensor(
                y[c][:, t, part], drop[c][t][:, part], 0.0, rise[t][:, cols], ALU.max, ALU.add
            )

        def store(c, t):
            nc.sync.dma_start(out_rows[:, t : t + 2, halves[c]], y[c][:, t : t + 2, :])

        y_words = sb("y_words", [P, S], U32)
        y_scales = sb("y_scales", [P, S], U8)
        out_words = out_1[0].rearrange("p n t -> p (n t)").bitcast(I32)

        def round_y(copy, c, part):
            copy(
                rounded[c][:, part, :].rearrange("p (n i) t -> p n t i", i=4),
                y[c][:, :, part].rearrange("p t (n i) -> p n t i", i=4),
            )

        for c in range(2):
            nc.scalar.activation(h2[0][:, halves[c]], acc2[0][c], ACT.Copy, scale=SIXTEENTH)
        for t in range(1, PACK):
            empty(t)
        for t in range(PACK):
            make_rise(t)
            if t > 0:
                finish(0, t - 1)
            fetch_low(0, t)
            make_drop(0, t)
            clip_rise(t)
        store(0, 0)
        last = PACK - 1
        for t in range(last):
            fetch_low(1, t)
            make_drop(1, t)
            if t == 0:
                finish(0, last)
                store(0, 2)
            else:
                finish(1, t - 1)
        fetch_low(1, last)
        parts = (slice(0, HALF // 2), slice(HALF // 2, HALF))
        round_y(nc.scalar.copy, 0, whole)
        finish(1, last - 1)
        store(1, 0)
        for part in parts:
            make_drop(1, last, part)
        for part in parts:
            finish(1, last, part)
        store(1, 2)
        for part in parts:
            round_y(nc.vector.tensor_copy, 1, part)
        for c in range(2):
            nc.vector.quantize_mx(
                out=y_words[:, halves[c]].bitcast(FP8X4),
                scales=y_scales[:, halves[c]],
                in_=rounded[c][:].rearrange("p n t -> p (n t)"),
            )
        nc.sync.dma_start(out_words, y_words[:].bitcast(I32))
        rows = QUADRANT // BLOCK_PARTITIONS
        for q in range(P // QUADRANT):
            queue = nc.scalar if q % 2 == 0 else nc.sync
            queue.dma_start(
                out_2[0, rows * q : rows * (q + 1), :].bitcast(I32),
                y_scales[QUADRANT * q : QUADRANT * q + rows, :].bitcast(I32),
            )
